import numpy as np
import ml_dtypes

BF16 = ml_dtypes.bfloat16


def bf(x):
    return np.asarray(x, np.float32).astype(BF16)


def f32(x):
    return np.asarray(x, np.float32)


def f64(x):
    return np.asarray(x).astype(np.float64)


def striped(idx):
    return np.tile(idx.reshape(-1, 16).T, (8, 1))


def rows(idx, k):
    return np.tile(idx, (k, 1))


def look(tab, idx):
    return np.take_along_axis(f64(tab), rows(idx, len(tab)), axis=1)


K, S, D, V, N, M = 128, 2048, 3, 512, 1536, 256


def setup_inputs():
    return {"tab": f32(np.random.standard_normal((K, S))), "th": f32(np.random.standard_normal((K, V))), "w": bf(np.random.standard_normal((K, M)) / np.sqrt(K)), "offs": striped(np.random.permutation(S)[:N])}


def reference(tab, th, w, offs):
    idx = offs[:16].T.reshape(-1)
    x = sum((look(tab, idx[d * V:(d + 1) * V]) >= f64(th)) * 1.0 for d in range(D)) / D
    y = f64(w).T @ x
    return y

@@ -1,0 +1,52 @@
+import concourse.mybir as mybir
+
+F32 = mybir.dt.float32
+BF16 = mybir.dt.bfloat16
+U16 = mybir.dt.uint16
+IS_GE = mybir.AluOpType.is_ge
+
+P = 128
+S = 2048
+VOTES = 3
+V = 512
+M = 256
+PER_COLUMN = 16
+
+FLOPS = 2 * P * M * V + VOTES * P * V
+
+
+def tile_lookup_vote_ge_none_kernel(tc, tab, th, w, offs, out):
+    nc = tc.nc
+    blocks = M // P
+    with (
+        tc.tile_pool(name="held", bufs=1) as held,
+        tc.tile_pool(name="work", bufs=VOTES) as work,
+        tc.psum_pool(name="psum", bufs=1) as psum,
+    ):
+        offsets = held.tile([P, VOTES * V // PER_COLUMN], U16, name="offsets")
+        table = held.tile([P, S], F32, name="table")
+        threshold = held.tile([P, V], F32, name="threshold")
+        weights = held.tile([P, M], BF16, name="weights")
+        nc.sync.dma_start(offsets[:], offs)
+        nc.scalar.dma_start(table[:], tab)
+        nc.sync.dma_start(threshold[:], th)
+        nc.scalar.dma_start(weights[:], w)
+
+        sums = [psum.tile([P, V], F32, name=f"sum{b}") for b in range(blocks)]
+        for d in range(VOTES):
+            first = d * V // PER_COLUMN
+            last = (d + 1) * V // PER_COLUMN
+            vote = work.tile([P, V], F32, name="vote")
+            nc.vector.tensor_tensor(vote[:], table[:].indirect(offsets[:, first:last]), threshold[:], IS_GE)
+            ballot = work.tile([P, V], BF16, name="ballot")
+            nc.scalar.copy(ballot[:], vote[:])
+            for b in range(blocks):
+                nc.tensor.matmul(
+                    sums[b][:], weights[:, b * P : (b + 1) * P], ballot[:], start=(d == 0), stop=(d == VOTES - 1)
+                )
+
+        result = [held.tile([P, V], F32, name=f"result{b}") for b in range(blocks)]
+        nc.scalar.mul(result[0][:], sums[0][:], 1.0 / VOTES)
+        nc.sync.dma_start(out[0:P, :], result[0][:])
+        nc.vector.tensor_scalar_mul(result[1][:], sums[1][:], 1.0 / VOTES)
+        nc.scalar.dma_start(out[P:M, :], result[1][:])

@@ -9,6 +9,8 @@ P = 128
 S = 2048
 VOTES = 3
 V = 512
+CHUNKS = 2
+C = V // CHUNKS
 M = 256
 PER_COLUMN = 16
 
@@ -21,7 +23,7 @@ def tile_lookup_vote_ge_none_kernel(tc, tab, th, w, offs, out):
     with (
         tc.tile_pool(name="held", bufs=1) as held,
         tc.tile_pool(name="work", bufs=VOTES) as work,
-        tc.psum_pool(name="psum", bufs=1) as psum,
+        tc.psum_pool(name="psum", bufs=2) as psum,
     ):
         offsets = held.tile([P, VOTES * V // PER_COLUMN], U16, name="offsets")
         table = held.tile([P, S], F32, name="table")
@@ -32,21 +34,25 @@ def tile_lookup_vote_ge_none_kernel(tc, tab, th, w, offs, out):
         nc.sync.dma_start(threshold[:], th)
         nc.scalar.dma_start(weights[:], w)
 
-        sums = [psum.tile([P, V], F32, name=f"sum{b}") for b in range(blocks)]
-        for d in range(VOTES):
-            first = d * V // PER_COLUMN
-            last = (d + 1) * V // PER_COLUMN
-            vote = work.tile([P, V], F32, name="vote")
-            nc.vector.tensor_tensor(vote[:], table[:].indirect(offsets[:, first:last]), threshold[:], IS_GE)
-            ballot = work.tile([P, V], BF16, name="ballot")
-            nc.scalar.copy(ballot[:], vote[:])
-            for b in range(blocks):
-                nc.tensor.matmul(
-                    sums[b][:], weights[:, b * P : (b + 1) * P], ballot[:], start=(d == 0), stop=(d == VOTES - 1)
-                )
+        for c in range(CHUNKS):
+            columns = slice(c * C, (c + 1) * C)
+            sums = [psum.tile([P, C], F32, name=f"sum{b}") for b in range(blocks)]
+            for d in range(VOTES):
+                first = (d * V + c * C) // PER_COLUMN
+                last = first + C // PER_COLUMN
+                vote = work.tile([P, C], F32, name="vote")
+                nc.vector.tensor_tensor(vote[:], table[:].indirect(offsets[:, first:last]), threshold[:, columns], IS_GE)
+                ballot = work.tile([P, C], BF16, name="ballot")
+                nc.scalar.copy(ballot[:], vote[:])
+                for b in range(blocks):
+                    nc.tensor.matmul(
+                        sums[b][:], weights[:, b * P : (b + 1) * P], ballot[:], start=(d == 0), stop=(d == VOTES - 1)
+                    )
 
-        result = [held.tile([P, V], F32, name=f"result{b}") for b in range(blocks)]
-        nc.scalar.mul(result[0][:], sums[0][:], 1.0 / VOTES)
-        nc.sync.dma_start(out[0:P, :], result[0][:])
-        nc.vector.tensor_scalar_mul(result[1][:], sums[1][:], 1.0 / VOTES)
-        nc.scalar.dma_start(out[P:M, :], result[1][:])
+            result = [work.tile([P, C], F32, name=f"result{b}") for b in range(blocks)]
+            for b in range(blocks):
+                if c == CHUNKS - 1 and b == blocks - 1:
+                    nc.vector.tensor_scalar_mul(result[b][:], sums[b][:], 1.0 / VOTES)
+                else:
+                    nc.scalar.mul(result[b][:], sums[b][:], 1.0 / VOTES)
+                nc.sync.dma_start(out[b * P : (b + 1) * P, columns], result[b][:])

@@ -27,12 +27,14 @@ def tile_lookup_vote_ge_none_kernel(tc, tab, th, w, offs, out):
     ):
         offsets = held.tile([P, VOTES * V // PER_COLUMN], U16, name="offsets")
         table = held.tile([P, S], F32, name="table")
-        threshold = held.tile([P, V], F32, name="threshold")
+        threshold = [held.tile([P, C], F32, name=f"threshold{c}") for c in range(CHUNKS)]
         weights = held.tile([P, M], BF16, name="weights")
         nc.sync.dma_start(offsets[:], offs)
+        nc.sync.dma_start(threshold[0][:], th[:, 0:C])
         nc.scalar.dma_start(table[:], tab)
-        nc.sync.dma_start(threshold[:], th)
         nc.scalar.dma_start(weights[:], w)
+        for c in range(1, CHUNKS):
+            nc.scalar.dma_start(threshold[c][:], th[:, c * C : (c + 1) * C])
 
         for c in range(CHUNKS):
             columns = slice(c * C, (c + 1) * C)
@@ -41,12 +43,11 @@ def tile_lookup_vote_ge_none_kernel(tc, tab, th, w, offs, out):
                 first = (d * V + c * C) // PER_COLUMN
                 last = first + C // PER_COLUMN
                 vote = work.tile([P, C], F32, name="vote")
-                nc.vector.tensor_tensor(vote[:], table[:].indirect(offsets[:, first:last]), threshold[:, columns], IS_GE)
-                ballot = work.tile([P, C], BF16, name="ballot")
-                nc.scalar.copy(ballot[:], vote[:])
+                nc.vector.tensor_tensor(vote[:], table[:].indirect(offsets[:, first:last]), threshold[c][:], IS_GE)
+                ballot = vote[:].bitcast(BF16)[:, 1 : 2 * C : 2]
                 for b in range(blocks):
                     nc.tensor.matmul(
-                        sums[b][:], weights[:, b * P : (b + 1) * P], ballot[:], start=(d == 0), stop=(d == VOTES - 1)
+                        sums[b][:], weights[:, b * P : (b + 1) * P], ballot, start=(d == 0), stop=(d == VOTES - 1)
                     )
 
             result = [work.tile([P, C], F32, name=f"result{b}") for b in range(blocks)]

import concourse.mybir as mybir

F32 = mybir.dt.float32
BF16 = mybir.dt.bfloat16
U16 = mybir.dt.uint16
IS_GE = mybir.AluOpType.is_ge

P = 128
S = 2048
VOTES = 3
V = 512
CHUNKS = 2
C = V // CHUNKS
M = 256
PER_COLUMN = 16

FLOPS = 2 * P * M * V + VOTES * P * V


def tile_lookup_vote_ge_none_kernel(tc, tab, th, w, offs, out):
    nc = tc.nc
    blocks = M // P
    with (
        tc.tile_pool(name="held", bufs=1) as held,
        tc.tile_pool(name="work", bufs=VOTES) as work,
        tc.psum_pool(name="psum", bufs=2) as psum,
    ):
        offsets = held.tile([P, VOTES * V // PER_COLUMN], U16, name="offsets")
        table = held.tile([P, S], F32, name="table")
        threshold = [held.tile([P, C], F32, name=f"threshold{c}") for c in range(CHUNKS)]
        weights = held.tile([P, M], BF16, name="weights")
        nc.sync.dma_start(offsets[:], offs)
        nc.sync.dma_start(threshold[0][:], th[:, 0:C])
        nc.scalar.dma_start(table[:], tab)
        nc.scalar.dma_start(weights[:], w)
        for c in range(1, CHUNKS):
            nc.scalar.dma_start(threshold[c][:], th[:, c * C : (c + 1) * C])

        for c in range(CHUNKS):
            columns = slice(c * C, (c + 1) * C)
            sums = [psum.tile([P, C], F32, name=f"sum{b}") for b in range(blocks)]
            for d in range(VOTES):
                first = (d * V + c * C) // PER_COLUMN
                last = first + C // PER_COLUMN
                vote = work.tile([P, C], F32, name="vote")
                nc.vector.tensor_tensor(vote[:], table[:].indirect(offsets[:, first:last]), threshold[c][:], IS_GE)
                ballot = vote[:].bitcast(BF16)[:, 1 : 2 * C : 2]
                for b in range(blocks):
                    nc.tensor.matmul(
                        sums[b][:], weights[:, b * P : (b + 1) * P], ballot, start=(d == 0), stop=(d == VOTES - 1)
                    )

            result = [work.tile([P, C], F32, name=f"result{b}") for b in range(blocks)]
            for b in range(blocks):
                if c == CHUNKS - 1 and b == blocks - 1:
                    nc.vector.tensor_scalar_mul(result[b][:], sums[b][:], 1.0 / VOTES)
                else:
                    nc.scalar.mul(result[b][:], sums[b][:], 1.0 / VOTES)
                nc.sync.dma_start(out[b * P : (b + 1) * P, columns], result[b][:])
